import numpy as np
import ml_dtypes


def mxq(x, axis, fmt="e4m3"):
    dtype, down = {"e4m3": (ml_dtypes.float8_e4m3fn, 7), "e5m2": (ml_dtypes.float8_e5m2, 14)}[fmt]
    v = np.moveaxis(np.asarray(x, np.float32).astype(ml_dtypes.bfloat16).astype(np.float64), axis, -1)
    blocks = v.reshape(v.shape[:-1] + (-1, 32))
    amax = np.abs(blocks).max(-1, keepdims=True)
    byte = np.maximum(np.where(amax > 0, np.frexp(amax)[1] - 1 + 127, 0) - down, 1)
    scale = np.exp2(byte - 127.0)
    codes = (blocks / scale).astype(np.float32).astype(dtype).astype(np.float64)
    return np.moveaxis((codes * scale).reshape(v.shape), -1, axis)


WIDE = False


def mx_kscale(k):
    if not WIDE:
        return np.ones(k)
    levels = np.array([10, -10, 5, -5, 0])
    if k % 512:
        return np.exp2(np.random.permutation(np.resize(levels, k // 32))).repeat(32)
    a = np.empty((k // 512, 16))
    for p in range(k // 512):
        a[p, :8] = np.random.permutation(np.resize(levels, 8))
        for g in range(8):
            far = levels[np.abs(levels - a[p, g]) >= 10]
            a[p, g + 8] = far[np.random.randint(len(far))]
    return np.exp2(a.ravel()).repeat(32)


def f64(x):
    return np.asarray(x).astype(np.float64)


def striped(idx):
    return np.tile(idx.reshape(-1, 16).T, (8, 1)).astype(np.uint16)


def unstriped(offs):
    return offs[:16].T.reshape(-1).astype(np.int64)


def striped8(idx):
    return np.concatenate([x.reshape(-1, 16).T for x in idx]).astype(np.uint16)


def runs(offs, k):
    lists = np.stack([offs[16 * r : 16 * r + 16].T.reshape(-1) for r in range(8)]).astype(np.int64)
    return lists[np.arange(k) % 512 // 64]


def pack_weight(w):
    k, n = w.shape
    w = f64(np.asarray(w, np.float32).astype(ml_dtypes.bfloat16)).reshape(k // 32, 32, n)
    amax = np.abs(w).max(1)
    byte = np.clip(np.where(amax > 0, np.frexp(amax)[1] - 1 + 127 - 7, 1), 1, 254)
    scaled = (w * np.exp2(127.0 - byte)[:, None, :]).reshape(k, n).astype(np.float32)
    words = np.ascontiguousarray(scaled.reshape(k // 512, 128, 4, n).transpose(0, 1, 3, 2)).astype(ml_dtypes.float8_e4m3fn).view(np.uint8)
    return words, np.ascontiguousarray(byte.astype(np.uint8).reshape(k // 512, 16, n))


def unpack_weight(words, scales):
    g, p, n, _ = words.shape
    vals = np.ascontiguousarray(words).view(ml_dtypes.float8_e4m3fn).astype(np.float64) * np.repeat(np.exp2(scales.astype(np.float64) - 127.0), 8, axis=1)[..., None]
    return vals.transpose(0, 1, 3, 2).reshape(g * 512, n)


E2M1 = np.array([0.0, 0.5, 1.0, 1.5, 2.0, 3.0, 4.0, 6.0, -0.0, -0.5, -1.0, -1.5, -2.0, -3.0, -4.0, -6.0])


def pack_fp4(w):
    k, n = w.shape
    w = f64(np.asarray(w, np.float32).astype(ml_dtypes.bfloat16)).reshape(k // 32, 32, n)
    amax = np.abs(w).max(1)
    mant, ex = np.frexp(amax / 6.0)
    byte = np.clip(np.where(amax > 0, np.where(mant > 0.5, ex, ex - 1) + 127, 1), 1, 254)
    scaled = (w * np.exp2(127.0 - byte)[:, None, :]).reshape(k, n).astype(np.float32)
    c = np.ascontiguousarray(scaled.reshape(k // 512, 128, 4, n).transpose(0, 1, 3, 2)).astype(ml_dtypes.float4_e2m1fn).view(np.uint8) & 0xF
    words = (c[..., 0::2] | (c[..., 1::2] << 4)).reshape(k // 512, 128, 2 * n)
    return np.ascontiguousarray(words), np.ascontiguousarray(byte.astype(np.uint8).reshape(k // 512, 16, n))


def unpack_fp4(words, scales):
    g, _, n = scales.shape
    words = np.ascontiguousarray(words).reshape(g, 128, n, 2)
    nib = np.empty((g, 128, n, 4), np.uint8)
    nib[..., 0::2] = words & 0xF
    nib[..., 1::2] = words >> 4
    vals = E2M1[nib] * np.repeat(np.exp2(scales.astype(np.float64) - 127.0), 8, axis=1)[..., None]
    return vals.transpose(0, 1, 3, 2).reshape(g * 512, n)


def planes(y):
    n, m = y.shape
    v = y.astype(np.float32).astype(ml_dtypes.bfloat16).astype(np.float64).reshape(n // 32, 32, m)
    top = np.abs(v).max(1)
    byte = np.clip(np.where(top > 0, np.frexp(top)[1] - 1 + 127 - 7, 1), 1, 254)
    codes = (v * np.exp2(127.0 - byte)[:, None, :]).reshape(n, m).astype(np.float32).astype(ml_dtypes.float8_e4m3fn).view(np.uint8)
    words = codes.reshape(n // 512, 128, 4, m).transpose(0, 1, 3, 2)
    return np.ascontiguousarray(words), np.ascontiguousarray(byte.astype(np.uint8).reshape(n // 512, 16, m))


K, T, S, V, N, G, H = 512, 2048, 512, 256, 512, 2048, 512


def setup_inputs():
    n = np.random.standard_normal
    s = mx_kscale(K)[:, None]
    u = mx_kscale(H)
    packed_xT = pack_weight(n((K, T)) * s)
    packed_dT = pack_weight(n((K, G)) / s)
    packed_w1 = pack_fp4(n((H, N)) / np.sqrt(H) / u[:, None])
    perm = np.stack([np.random.permutation(S) for _ in range(8)])
    return {
        "x_words": packed_xT[0],
        "x_scales": packed_xT[1],
        "d_words": packed_dT[0],
        "d_scales": packed_dT[1],
        "gn": (np.random.uniform(0.5, 1.5, (H, 1)) * u[:, None]).astype(np.float32),
        "w1_words": packed_w1[0],
        "w1_scales": packed_w1[1],
        "offs": striped(np.random.permutation(T)[:S]),
        "kidx": striped8(np.random.randint(0, G, (8, H))),
        "la": striped8(perm[:, :V]),
        "lb": striped8(perm[:, V:]),
    }


def reference(x_words, x_scales, d_words, d_scales, gn, w1_words, w1_scales, offs, kidx, la, lb):
    d_kidx = unpack_weight(d_words, d_scales)[np.arange(K)[:, None], runs(kidx, K)]
    xq = unpack_weight(x_words, x_scales)[:, unstriped(offs)]
    s = 0.0625 * (d_kidx.T @ xq)
    a = s[np.arange(H)[:, None], runs(la, H)]
    b = s[np.arange(H)[:, None], runs(lb, H)]
    lo = np.minimum(a, b)
    hi = np.maximum(a, b)
    sp = np.zeros((H, S))
    sp[np.arange(H)[:, None], runs(la, H)] = hi
    sd = sp.copy()
    sd[np.arange(H)[:, None], runs(lb, H)] = lo
    z = f64(gn) * sd
    out_0 = unpack_fp4(w1_words, w1_scales).T @ mxq(z, 0, "e4m3")
    return (out_0,) + planes(out_0)

@@ -1,0 +1,199 @@
+from contextlib import ExitStack
+
+import concourse.mybir as mybir
+
+K, T, S, V, N, G, H = 512, 2048, 512, 256, 512, 2048, 512
+FLOPS = 2 * K * H * S + 2 * H * N * S
+
+F32 = mybir.dt.float32
+BF16 = mybir.dt.bfloat16
+I32 = mybir.dt.int32
+U32 = mybir.dt.uint32
+U16 = mybir.dt.uint16
+U8 = mybir.dt.uint8
+FP8X4 = mybir.dt.float8_e4m3fn_x4
+FP4X4 = mybir.dt.float4_e2m1fn_x4
+COPY = mybir.ActivationFunctionType.Copy
+ALU = mybir.AluOpType
+
+P = 128
+PACK = 4
+QUAD = 32
+CHUNK = 128
+SCORE_SCALE = 0.0625
+
+
+def tile_picked_scoreord_none_po_kernel(
+    tc, x_words, x_scales, d_words, d_scales, gn, w1_words, w1_scales, offs, kidx, la, lb, out_0, out_1, out_2
+):
+    nc = tc.nc
+    with ExitStack() as ctx:
+        lists = ctx.enter_context(tc.tile_pool(name="lists", bufs=1))
+        keep = ctx.enter_context(tc.tile_pool(name="keep", bufs=1))
+        psum = ctx.enter_context(tc.psum_pool(name="psum", bufs=1))
+
+        kidx_sb = lists.tile([P, H // 16], U16, name="kidx_sb")
+        offs_sb = lists.tile([P, S // 16], U16, name="offs_sb")
+        la_sb = lists.tile([P, V // 16], U16, name="la_sb")
+        lb_sb = lists.tile([P, V // 16], U16, name="lb_sb")
+
+        d_table = keep.tile([P, G], U32, name="d_table")
+        x_table = keep.tile([P, T], U32, name="x_table")
+        d_table_sc = keep.tile([P, G], U8, name="d_table_sc")
+        x_table_sc = keep.tile([P, T], U8, name="x_table_sc")
+        d_sc = keep.tile([P, H], U8, name="d_sc", align_bytes=64)
+        w_raw_sc = keep.tile([P, N], U8, name="w_raw_sc")
+        gn_raw = keep.tile([P, PACK], F32, name="gn_raw")
+
+        nc.vector.memset(d_table_sc[:].bitcast(I32), 0)
+        nc.vector.memset(x_table_sc[:].bitcast(I32), 0)
+        nc.gpsimd.memset(w_raw_sc[:].bitcast(I32), 0)
+        nc.gpsimd.memset(d_sc[:].bitcast(I32), 0)
+
+        nc.sync.dma_start(kidx_sb[:], kidx)
+        nc.scalar.dma_start(d_table_sc[0:P:8, :].bitcast(I32), d_scales[0].bitcast(I32))
+        nc.sync.dma_start(d_table[:].bitcast(I32), d_words[0].rearrange("p n t -> p (n t)").bitcast(I32))
+        nc.sync.dma_start(offs_sb[:], offs)
+        nc.sync.dma_start(la_sb[:], la)
+        nc.sync.dma_start(lb_sb[:], lb)
+        for q in range(PACK):
+            nc.scalar.dma_start(
+                x_table_sc[QUAD * q : QUAD * q + 4, :].bitcast(I32), x_scales[0, 4 * q : 4 * q + 4, :].bitcast(I32)
+            )
+        nc.sync.dma_start(x_table[:].bitcast(I32), x_words[0].rearrange("p n t -> p (n t)").bitcast(I32))
+        nc.gpsimd.dma_start(gn_raw[:], gn.rearrange("(p t) o -> p (t o)", t=PACK))
+        for q in range(PACK):
+            nc.gpsimd.dma_start(
+                w_raw_sc[QUAD * q : QUAD * q + 4, :].bitcast(I32), w1_scales[0, 4 * q : 4 * q + 4, :].bitcast(I32)
+            )
+
+        gain = keep.tile([P, PACK], F32, name="gain")
+        nc.scalar.activation(gain[:], gn_raw[:], COPY, scale=SCORE_SCALE)
+
+        d_picked_sc = keep.tile([P, H], U8, name="d_picked_sc")
+        nc.vector.tensor_copy(d_picked_sc[:], d_table_sc[:].indirect(kidx_sb[:]))
+        d_dealt_sc = keep.tile([P, H], U8, name="d_dealt_sc", tag="staged")
+        nc.vector.tensor_copy(
+            d_dealt_sc[:].rearrange("p (t c i) -> p c t i", t=PACK, i=16),
+            d_picked_sc[:].rearrange("p (c i t) -> p c t i", t=PACK, i=16),
+        )
+        for r in range(4):
+            nc.sync.dma_start(d_sc[r:P:QUAD, :].bitcast(I32), d_dealt_sc[8 * r : P : QUAD, :].bitcast(I32))
+
+        d_picked = keep.tile([P, H], U32, name="d_picked")
+        nc.vector.tensor_copy(d_picked[:], d_table[:].indirect(kidx_sb[:]))
+        x_sc = keep.tile([P, S], U8, name="x_sc", align_bytes=64)
+        nc.vector.tensor_copy(x_sc[:], x_table_sc[:].indirect(offs_sb[:]))
+        d_codes = keep.tile([P, H], U32, name="d_codes", align_bytes=64)
+        nc.vector.tensor_copy(
+            d_codes[:].rearrange("p (t c i) -> p c t i", t=PACK, i=4),
+            d_picked[:].rearrange("p (c i t) -> p c t i", t=PACK, i=4),
+        )
+        x_codes = keep.tile([P, S], U32, name="x_codes", align_bytes=64)
+        nc.vector.tensor_copy(x_codes[:], x_table[:].indirect(offs_sb[:]))
+
+        w_raw = keep.tile([P, 2 * N], U8, name="w_raw", tag="staged")
+        nc.sync.dma_start(w_raw[:].bitcast(I32), w1_words[0].bitcast(I32))
+        w_codes = keep.tile([P, 2 * N], U8, name="w_codes", align_bytes=64)
+        nc.vector.tensor_copy(
+            w_codes[:].rearrange("p (t c i b) -> p c t i b", t=PACK, i=8, b=2),
+            w_raw[:].rearrange("p (c i t b) -> p c t i b", t=PACK, i=8, b=2),
+        )
+        w_sc = keep.tile([P, N], U8, name="w_sc", align_bytes=64)
+        nc.vector.tensor_copy(
+            w_sc[:].rearrange("p (t c i) -> p c t i", t=PACK, i=16),
+            w_raw_sc[:].rearrange("p (c i t) -> p c t i", t=PACK, i=16),
+        )
+
+        a = keep.tile([P, PACK, V], F32, name="a")
+        b = keep.tile([P, PACK, V], F32, name="b")
+        hi = keep.tile([P, PACK, V], F32, name="hi")
+        lo = keep.tile([P, PACK, V], F32, name="lo")
+        for t in range(PACK):
+            cols = slice(t * P, (t + 1) * P)
+            acc = psum.tile([P, S], F32, name="score_bank%d" % t)
+            nc.tensor.matmul_mx(
+                out=acc[:],
+                lhsT=d_codes[:, cols].bitcast(FP8X4),
+                lhsT_scale=d_sc[:, cols],
+                rhs=x_codes[:].bitcast(FP8X4),
+                rhs_scale=x_sc[:],
+                start=True,
+                stop=True,
+            )
+            score = keep.tile([P, S], F32, name="score%d" % t)
+            nc.scalar.copy(score[:], acc[:])
+            nc.vector.tensor_copy(a[:, t, :], score[:].indirect(la_sb[:]))
+            nc.vector.tensor_copy(b[:, t, :], score[:].indirect(lb_sb[:]))
+        for h in range(2):
+            pair = slice(2 * h, 2 * h + 2)
+            nc.vector.tensor_tensor(hi[:, pair, :], a[:, pair, :], b[:, pair, :], ALU.max)
+            nc.vector.tensor_tensor(lo[:, pair, :], a[:, pair, :], b[:, pair, :], ALU.min)
+
+        ordered = [keep.tile([P, S], F32, name="ordered%d" % t) for t in range(PACK)]
+        z = keep.tile([P, S, PACK], BF16, name="z", align_bytes=64)
+
+        def put_hi(t):
+            nc.vector.tensor_copy(ordered[t][:].indirect(la_sb[:]), hi[:, t, :])
+
+        def put_lo(t):
+            nc.vector.tensor_copy(ordered[t][:].indirect(lb_sb[:]), lo[:, t, :])
+
+        def weigh(t, cols):
+            nc.scalar.activation(z[:, cols, t], ordered[t][:, cols], COPY, scale=gain[:, t : t + 1])
+
+        put_hi(0)
+        for t in range(PACK):
+            if t + 1 < PACK:
+                put_hi(t + 1)
+            put_lo(t)
+            if t + 1 < PACK:
+                weigh(t, slice(0, S))
+
+        z_codes = keep.tile([P, S], U32, name="z_codes", align_bytes=64)
+        z_sc = keep.tile([P, S], U8, name="z_sc", align_bytes=64)
+        y_codes = keep.tile([P, S], U32, name="y_codes", align_bytes=64)
+        y_sc = keep.tile([P, S], U8, name="y_sc", align_bytes=64)
+        out_rows = out_0.rearrange("(p t) j -> p t j", t=PACK)
+        out_words = out_1[0].rearrange("p n t -> p (n t)").bitcast(I32)
+        chunks = [slice(c, c + CHUNK) for c in range(0, S, CHUNK)]
+        for cols in chunks:
+            weigh(PACK - 1, cols)
+            nc.vector.quantize_mx(
+                out=z_codes[:, cols].bitcast(FP8X4),
+                scales=z_sc[:, cols],
+                in_=z[:, cols, :].rearrange("p j t -> p (j t)"),
+            )
+        for c, cols in enumerate(chunks):
+            y_bank = psum.tile([P, PACK, CHUNK], F32, name="y_bank%d" % c)
+            for t in range(PACK):
+                nc.tensor.matmul_mx(
+                    out=y_bank[:, t, :],
+                    lhsT=w_codes[:, 2 * t * P : 2 * (t + 1) * P].bitcast(FP4X4),
+                    lhsT_scale=w_sc[:, t * P : (t + 1) * P],
+                    rhs=z_codes[:, cols].bitcast(FP8X4),
+                    rhs_scale=z_sc[:, cols],
+                    start=True,
+                    stop=True,
+                )
+            y = keep.tile([P, PACK, CHUNK], F32, name="y%d" % c)
+            nc.scalar.copy(y[:], y_bank[:])
+            nc.sync.dma_start(out_rows[:, :, cols], y[:])
+            y_rounded = keep.tile([P, CHUNK, PACK], BF16, name="y_rounded%d" % c, align_bytes=64)
+            nc.vector.tensor_copy(
+                y_rounded[:].rearrange("p (c i) t -> p c t i", i=4),
+                y[:].rearrange("p t (c i) -> p c t i", i=4),
+            )
+            nc.vector.quantize_mx(
+                out=y_codes[:, cols].bitcast(FP8X4),
+                scales=y_sc[:, cols],
+                in_=y_rounded[:].rearrange("p j t -> p (j t)"),
+            )
+            if c % 2 == 1:
+                half = slice(cols.start - CHUNK, cols.stop)
+                nc.sync.dma_start(out_words[:, half], y_codes[:, half].bitcast(I32))
+        for q in range(PACK):
+            queue = nc.scalar if q % 2 else nc.sync
+            queue.dma_start(
+                out_2[0, 4 * q : 4 * q + 4, :].bitcast(I32), y_sc[QUAD * q : QUAD * q + 4, :].bitcast(I32)
+            )

@@ -30,6 +30,7 @@ def tile_picked_scoreord_none_po_kernel(
     with ExitStack() as ctx:
         lists = ctx.enter_context(tc.tile_pool(name="lists", bufs=1))
         keep = ctx.enter_context(tc.tile_pool(name="keep", bufs=1))
+        reuse = ctx.enter_context(tc.tile_pool(name="reuse", bufs=1))
         psum = ctx.enter_context(tc.psum_pool(name="psum", bufs=1))
 
         kidx_sb = lists.tile([P, H // 16], U16, name="kidx_sb")
@@ -38,28 +39,29 @@ def tile_picked_scoreord_none_po_kernel(
         lb_sb = lists.tile([P, V // 16], U16, name="lb_sb")
 
         d_table = keep.tile([P, G], U32, name="d_table")
-        x_table = keep.tile([P, T], U32, name="x_table")
+        x_table = reuse.tile([P, T], U32, name="x_table", offset=0)
         d_table_sc = keep.tile([P, G], U8, name="d_table_sc")
         x_table_sc = keep.tile([P, T], U8, name="x_table_sc")
         d_sc = keep.tile([P, H], U8, name="d_sc", align_bytes=64)
         w_raw_sc = keep.tile([P, N], U8, name="w_raw_sc")
         gn_raw = keep.tile([P, PACK], F32, name="gn_raw")
 
-        nc.vector.memset(d_table_sc[:].bitcast(I32), 0)
-        nc.vector.memset(x_table_sc[:].bitcast(I32), 0)
-        nc.gpsimd.memset(w_raw_sc[:].bitcast(I32), 0)
-        nc.gpsimd.memset(d_sc[:].bitcast(I32), 0)
+        nc.gpsimd.memset(x_table_sc[:].bitcast(I32), 0)
+        nc.vector.memset(w_raw_sc[:].bitcast(I32), 0)
+        nc.vector.memset(d_sc[:].bitcast(I32), 0)
 
+        nc.scalar.dma_start(
+            d_table_sc[:].bitcast(I32), d_scales[0].bitcast(I32).unsqueeze(1).broadcast_to([16, 8, G // 4])
+        )
         nc.sync.dma_start(kidx_sb[:], kidx)
-        nc.scalar.dma_start(d_table_sc[0:P:8, :].bitcast(I32), d_scales[0].bitcast(I32))
-        nc.sync.dma_start(d_table[:].bitcast(I32), d_words[0].rearrange("p n t -> p (n t)").bitcast(I32))
         nc.sync.dma_start(offs_sb[:], offs)
-        nc.sync.dma_start(la_sb[:], la)
-        nc.sync.dma_start(lb_sb[:], lb)
+        nc.sync.dma_start(d_table[:].bitcast(I32), d_words[0].rearrange("p n t -> p (n t)").bitcast(I32))
         for q in range(PACK):
-            nc.scalar.dma_start(
+            nc.sync.dma_start(
                 x_table_sc[QUAD * q : QUAD * q + 4, :].bitcast(I32), x_scales[0, 4 * q : 4 * q + 4, :].bitcast(I32)
             )
+        nc.sync.dma_start(la_sb[:], la)
+        nc.sync.dma_start(lb_sb[:], lb)
         nc.sync.dma_start(x_table[:].bitcast(I32), x_words[0].rearrange("p n t -> p (n t)").bitcast(I32))
         nc.gpsimd.dma_start(gn_raw[:], gn.rearrange("(p t) o -> p (t o)", t=PACK))
         for q in range(PACK):
@@ -90,16 +92,18 @@ def tile_picked_scoreord_none_po_kernel(
             d_picked[:].rearrange("p (c i t) -> p c t i", t=PACK, i=4),
         )
         x_codes = keep.tile([P, S], U32, name="x_codes", align_bytes=64)
-        nc.vector.tensor_copy(x_codes[:], x_table[:].indirect(offs_sb[:]))
+        halves = [slice(0, S // 2), slice(S // 2, S)]
+        for half in halves:
+            nc.vector.tensor_copy(x_codes[:, half], x_table[:].indirect(offs_sb[:, half.start // 16 : half.stop // 16]))
 
         w_raw = keep.tile([P, 2 * N], U8, name="w_raw", tag="staged")
         nc.sync.dma_start(w_raw[:].bitcast(I32), w1_words[0].bitcast(I32))
-        w_codes = keep.tile([P, 2 * N], U8, name="w_codes", align_bytes=64)
+        w_codes = reuse.tile([P, 2 * N], U8, name="w_codes", align_bytes=64, offset=0)
         nc.vector.tensor_copy(
             w_codes[:].rearrange("p (t c i b) -> p c t i b", t=PACK, i=8, b=2),
             w_raw[:].rearrange("p (c i t b) -> p c t i b", t=PACK, i=8, b=2),
         )
-        w_sc = keep.tile([P, N], U8, name="w_sc", align_bytes=64)
+        w_sc = reuse.tile([P, N], U8, name="w_sc", align_bytes=64, offset=2 * N)
         nc.vector.tensor_copy(
             w_sc[:].rearrange("p (t c i) -> p c t i", t=PACK, i=16),
             w_raw_sc[:].rearrange("p (c i t) -> p c t i", t=PACK, i=16),
@@ -109,22 +113,23 @@ def tile_picked_scoreord_none_po_kernel(
         b = keep.tile([P, PACK, V], F32, name="b")
         hi = keep.tile([P, PACK, V], F32, name="hi")
         lo = keep.tile([P, PACK, V], F32, name="lo")
+        score = [keep.tile([P, S], F32, name="score%d" % t) for t in range(PACK)]
         for t in range(PACK):
             cols = slice(t * P, (t + 1) * P)
-            acc = psum.tile([P, S], F32, name="score_bank%d" % t)
-            nc.tensor.matmul_mx(
-                out=acc[:],
-                lhsT=d_codes[:, cols].bitcast(FP8X4),
-                lhsT_scale=d_sc[:, cols],
-                rhs=x_codes[:].bitcast(FP8X4),
-                rhs_scale=x_sc[:],
-                start=True,
-                stop=True,
-            )
-            score = keep.tile([P, S], F32, name="score%d" % t)
-            nc.scalar.copy(score[:], acc[:])
-            nc.vector.tensor_copy(a[:, t, :], score[:].indirect(la_sb[:]))
-            nc.vector.tensor_copy(b[:, t, :], score[:].indirect(lb_sb[:]))
+            for h, half in enumerate(halves):
+                acc = psum.tile([P, S // 2], F32, name="acc", tag="bank%d" % (2 * t + h))
+                nc.tensor.matmul_mx(
+                    out=acc[:],
+                    lhsT=d_codes[:, cols].bitcast(FP8X4),
+                    lhsT_scale=d_sc[:, cols],
+                    rhs=x_codes[:, half].bitcast(FP8X4),
+                    rhs_scale=x_sc[:, half],
+                    start=True,
+                    stop=True,
+                )
+                nc.scalar.copy(score[t][:, half], acc[:])
+            nc.vector.tensor_copy(a[:, t, :], score[t][:].indirect(la_sb[:]))
+            nc.vector.tensor_copy(b[:, t, :], score[t][:].indirect(lb_sb[:]))
         for h in range(2):
             pair = slice(2 * h, 2 * h + 2)
             nc.vector.tensor_tensor(hi[:, pair, :], a[:, pair, :], b[:, pair, :], ALU.max)
@@ -165,19 +170,24 @@ def tile_picked_scoreord_none_po_kernel(
                 in_=z[:, cols, :].rearrange("p j t -> p (j t)"),
             )
         for c, cols in enumerate(chunks):
-            y_bank = psum.tile([P, PACK, CHUNK], F32, name="y_bank%d" % c)
-            for t in range(PACK):
-                nc.tensor.matmul_mx(
-                    out=y_bank[:, t, :],
-                    lhsT=w_codes[:, 2 * t * P : 2 * (t + 1) * P].bitcast(FP4X4),
-                    lhsT_scale=w_sc[:, t * P : (t + 1) * P],
-                    rhs=z_codes[:, cols].bitcast(FP8X4),
-                    rhs_scale=z_sc[:, cols],
-                    start=True,
-                    stop=True,
-                )
             y = keep.tile([P, PACK, CHUNK], F32, name="y%d" % c)
-            nc.scalar.copy(y[:], y_bank[:])
+            for h in range(2):
+                y_bank = psum.tile([P, 2, CHUNK], F32, name="y_bank", tag="bank%d" % (2 * c + h))
+                for u in range(2):
+                    t = 2 * h + u
+                    nc.tensor.matmul_mx(
+                        out=y_bank[:, u, :],
+                        lhsT=w_codes[:, 2 * t * P : 2 * (t + 1) * P].bitcast(FP4X4),
+                        lhsT_scale=w_sc[:, t * P : (t + 1) * P],
+                        rhs=z_codes[:, cols].bitcast(FP8X4),
+                        rhs_scale=z_sc[:, cols],
+                        start=True,
+                        stop=True,
+                    )
+                if c == 0:
+                    nc.vector.tensor_copy(y[:, 2 * h : 2 * h + 2, :], y_bank[:])
+                else:
+                    nc.scalar.copy(y[:, 2 * h : 2 * h + 2, :], y_bank[:])
             nc.sync.dma_start(out_rows[:, :, cols], y[:])
             y_rounded = keep.tile([P, CHUNK, PACK], BF16, name="y_rounded%d" % c, align_bytes=64)
             nc.vector.tensor_copy(
@@ -189,11 +199,11 @@ def tile_picked_scoreord_none_po_kernel(
                 scales=y_sc[:, cols],
                 in_=y_rounded[:].rearrange("p j t -> p (j t)"),
             )
-            if c % 2 == 1:
-                half = slice(cols.start - CHUNK, cols.stop)
-                nc.sync.dma_start(out_words[:, half], y_codes[:, half].bitcast(I32))
+            if c >= len(chunks) - 2:
+                done = slice(0, cols.stop) if c == len(chunks) - 2 else cols
+                nc.sync.dma_start(out_words[:, done], y_codes[:, done].bitcast(I32))
         for q in range(PACK):
-            queue = nc.scalar if q % 2 else nc.sync
+            queue = nc.scalar if q else nc.sync
             queue.dma_start(
                 out_2[0, 4 * q : 4 * q + 4, :].bitcast(I32), y_sc[QUAD * q : QUAD * q + 4, :].bitcast(I32)
             )

from contextlib import ExitStack

import concourse.mybir as mybir

K, T, S, V, N, G, H = 512, 2048, 512, 256, 512, 2048, 512
FLOPS = 2 * K * H * S + 2 * H * N * S

F32 = mybir.dt.float32
BF16 = mybir.dt.bfloat16
I32 = mybir.dt.int32
U32 = mybir.dt.uint32
U16 = mybir.dt.uint16
U8 = mybir.dt.uint8
FP8X4 = mybir.dt.float8_e4m3fn_x4
FP4X4 = mybir.dt.float4_e2m1fn_x4
COPY = mybir.ActivationFunctionType.Copy
ALU = mybir.AluOpType

P = 128
PACK = 4
QUAD = 32
CHUNK = 128
SCORE_SCALE = 0.0625


def tile_picked_scoreord_none_po_kernel(
    tc, x_words, x_scales, d_words, d_scales, gn, w1_words, w1_scales, offs, kidx, la, lb, out_0, out_1, out_2
):
    nc = tc.nc
    with ExitStack() as ctx:
        lists = ctx.enter_context(tc.tile_pool(name="lists", bufs=1))
        keep = ctx.enter_context(tc.tile_pool(name="keep", bufs=1))
        reuse = ctx.enter_context(tc.tile_pool(name="reuse", bufs=1))
        psum = ctx.enter_context(tc.psum_pool(name="psum", bufs=1))

        kidx_sb = lists.tile([P, H // 16], U16, name="kidx_sb")
        offs_sb = lists.tile([P, S // 16], U16, name="offs_sb")
        la_sb = lists.tile([P, V // 16], U16, name="la_sb")
        lb_sb = lists.tile([P, V // 16], U16, name="lb_sb")

        d_table = keep.tile([P, G], U32, name="d_table")
        x_table = reuse.tile([P, T], U32, name="x_table", offset=0)
        d_table_sc = keep.tile([P, G], U8, name="d_table_sc")
        x_table_sc = keep.tile([P, T], U8, name="x_table_sc")
        d_sc = keep.tile([P, H], U8, name="d_sc", align_bytes=64)
        w_raw_sc = keep.tile([P, N], U8, name="w_raw_sc")
        gn_raw = keep.tile([P, PACK], F32, name="gn_raw")

        nc.gpsimd.memset(x_table_sc[:].bitcast(I32), 0)
        nc.vector.memset(w_raw_sc[:].bitcast(I32), 0)
        nc.vector.memset(d_sc[:].bitcast(I32), 0)

        nc.scalar.dma_start(
            d_table_sc[:].bitcast(I32), d_scales[0].bitcast(I32).unsqueeze(1).broadcast_to([16, 8, G // 4])
        )
        nc.sync.dma_start(kidx_sb[:], kidx)
        nc.sync.dma_start(offs_sb[:], offs)
        nc.sync.dma_start(d_table[:].bitcast(I32), d_words[0].rearrange("p n t -> p (n t)").bitcast(I32))
        for q in range(PACK):
            nc.sync.dma_start(
                x_table_sc[QUAD * q : QUAD * q + 4, :].bitcast(I32), x_scales[0, 4 * q : 4 * q + 4, :].bitcast(I32)
            )
        nc.sync.dma_start(la_sb[:], la)
        nc.sync.dma_start(lb_sb[:], lb)
        nc.sync.dma_start(x_table[:].bitcast(I32), x_words[0].rearrange("p n t -> p (n t)").bitcast(I32))
        nc.gpsimd.dma_start(gn_raw[:], gn.rearrange("(p t) o -> p (t o)", t=PACK))
        for q in range(PACK):
            nc.gpsimd.dma_start(
                w_raw_sc[QUAD * q : QUAD * q + 4, :].bitcast(I32), w1_scales[0, 4 * q : 4 * q + 4, :].bitcast(I32)
            )

        gain = keep.tile([P, PACK], F32, name="gain")
        nc.scalar.activation(gain[:], gn_raw[:], COPY, scale=SCORE_SCALE)

        d_picked_sc = keep.tile([P, H], U8, name="d_picked_sc")
        nc.vector.tensor_copy(d_picked_sc[:], d_table_sc[:].indirect(kidx_sb[:]))
        d_dealt_sc = keep.tile([P, H], U8, name="d_dealt_sc", tag="staged")
        nc.vector.tensor_copy(
            d_dealt_sc[:].rearrange("p (t c i) -> p c t i", t=PACK, i=16),
            d_picked_sc[:].rearrange("p (c i t) -> p c t i", t=PACK, i=16),
        )
        for r in range(4):
            nc.sync.dma_start(d_sc[r:P:QUAD, :].bitcast(I32), d_dealt_sc[8 * r : P : QUAD, :].bitcast(I32))

        d_picked = keep.tile([P, H], U32, name="d_picked")
        nc.vector.tensor_copy(d_picked[:], d_table[:].indirect(kidx_sb[:]))
        x_sc = keep.tile([P, S], U8, name="x_sc", align_bytes=64)
        nc.vector.tensor_copy(x_sc[:], x_table_sc[:].indirect(offs_sb[:]))
        d_codes = keep.tile([P, H], U32, name="d_codes", align_bytes=64)
        nc.vector.tensor_copy(
            d_codes[:].rearrange("p (t c i) -> p c t i", t=PACK, i=4),
            d_picked[:].rearrange("p (c i t) -> p c t i", t=PACK, i=4),
        )
        x_codes = keep.tile([P, S], U32, name="x_codes", align_bytes=64)
        halves = [slice(0, S // 2), slice(S // 2, S)]
        for half in halves:
            nc.vector.tensor_copy(x_codes[:, half], x_table[:].indirect(offs_sb[:, half.start // 16 : half.stop // 16]))

        w_raw = keep.tile([P, 2 * N], U8, name="w_raw", tag="staged")
        nc.sync.dma_start(w_raw[:].bitcast(I32), w1_words[0].bitcast(I32))
        w_codes = reuse.tile([P, 2 * N], U8, name="w_codes", align_bytes=64, offset=0)
        nc.vector.tensor_copy(
            w_codes[:].rearrange("p (t c i b) -> p c t i b", t=PACK, i=8, b=2),
            w_raw[:].rearrange("p (c i t b) -> p c t i b", t=PACK, i=8, b=2),
        )
        w_sc = reuse.tile([P, N], U8, name="w_sc", align_bytes=64, offset=2 * N)
        nc.vector.tensor_copy(
            w_sc[:].rearrange("p (t c i) -> p c t i", t=PACK, i=16),
            w_raw_sc[:].rearrange("p (c i t) -> p c t i", t=PACK, i=16),
        )

        a = keep.tile([P, PACK, V], F32, name="a")
        b = keep.tile([P, PACK, V], F32, name="b")
        hi = keep.tile([P, PACK, V], F32, name="hi")
        lo = keep.tile([P, PACK, V], F32, name="lo")
        score = [keep.tile([P, S], F32, name="score%d" % t) for t in range(PACK)]
        for t in range(PACK):
            cols = slice(t * P, (t + 1) * P)
            for h, half in enumerate(halves):
                acc = psum.tile([P, S // 2], F32, name="acc", tag="bank%d" % (2 * t + h))
                nc.tensor.matmul_mx(
                    out=acc[:],
                    lhsT=d_codes[:, cols].bitcast(FP8X4),
                    lhsT_scale=d_sc[:, cols],
                    rhs=x_codes[:, half].bitcast(FP8X4),
                    rhs_scale=x_sc[:, half],
                    start=True,
                    stop=True,
                )
                nc.scalar.copy(score[t][:, half], acc[:])
            nc.vector.tensor_copy(a[:, t, :], score[t][:].indirect(la_sb[:]))
            nc.vector.tensor_copy(b[:, t, :], score[t][:].indirect(lb_sb[:]))
        for h in range(2):
            pair = slice(2 * h, 2 * h + 2)
            nc.vector.tensor_tensor(hi[:, pair, :], a[:, pair, :], b[:, pair, :], ALU.max)
            nc.vector.tensor_tensor(lo[:, pair, :], a[:, pair, :], b[:, pair, :], ALU.min)

        ordered = [keep.tile([P, S], F32, name="ordered%d" % t) for t in range(PACK)]
        z = keep.tile([P, S, PACK], BF16, name="z", align_bytes=64)

        def put_hi(t):
            nc.vector.tensor_copy(ordered[t][:].indirect(la_sb[:]), hi[:, t, :])

        def put_lo(t):
            nc.vector.tensor_copy(ordered[t][:].indirect(lb_sb[:]), lo[:, t, :])

        def weigh(t, cols):
            nc.scalar.activation(z[:, cols, t], ordered[t][:, cols], COPY, scale=gain[:, t : t + 1])

        put_hi(0)
        for t in range(PACK):
            if t + 1 < PACK:
                put_hi(t + 1)
            put_lo(t)
            if t + 1 < PACK:
                weigh(t, slice(0, S))

        z_codes = keep.tile([P, S], U32, name="z_codes", align_bytes=64)
        z_sc = keep.tile([P, S], U8, name="z_sc", align_bytes=64)
        y_codes = keep.tile([P, S], U32, name="y_codes", align_bytes=64)
        y_sc = keep.tile([P, S], U8, name="y_sc", align_bytes=64)
        out_rows = out_0.rearrange("(p t) j -> p t j", t=PACK)
        out_words = out_1[0].rearrange("p n t -> p (n t)").bitcast(I32)
        chunks = [slice(c, c + CHUNK) for c in range(0, S, CHUNK)]
        for cols in chunks:
            weigh(PACK - 1, cols)
            nc.vector.quantize_mx(
                out=z_codes[:, cols].bitcast(FP8X4),
                scales=z_sc[:, cols],
                in_=z[:, cols, :].rearrange("p j t -> p (j t)"),
            )
        for c, cols in enumerate(chunks):
            y = keep.tile([P, PACK, CHUNK], F32, name="y%d" % c)
            for h in range(2):
                y_bank = psum.tile([P, 2, CHUNK], F32, name="y_bank", tag="bank%d" % (2 * c + h))
                for u in range(2):
                    t = 2 * h + u
                    nc.tensor.matmul_mx(
                        out=y_bank[:, u, :],
                        lhsT=w_codes[:, 2 * t * P : 2 * (t + 1) * P].bitcast(FP4X4),
                        lhsT_scale=w_sc[:, t * P : (t + 1) * P],
                        rhs=z_codes[:, cols].bitcast(FP8X4),
                        rhs_scale=z_sc[:, cols],
                        start=True,
                        stop=True,
                    )
                if c == 0:
                    nc.vector.tensor_copy(y[:, 2 * h : 2 * h + 2, :], y_bank[:])
                else:
                    nc.scalar.copy(y[:, 2 * h : 2 * h + 2, :], y_bank[:])
            nc.sync.dma_start(out_rows[:, :, cols], y[:])
            y_rounded = keep.tile([P, CHUNK, PACK], BF16, name="y_rounded%d" % c, align_bytes=64)
            nc.vector.tensor_copy(
                y_rounded[:].rearrange("p (c i) t -> p c t i", i=4),
                y[:].rearrange("p t (c i) -> p c t i", i=4),
            )
            nc.vector.quantize_mx(
                out=y_codes[:, cols].bitcast(FP8X4),
                scales=y_sc[:, cols],
                in_=y_rounded[:].rearrange("p j t -> p (j t)"),
            )
            if c >= len(chunks) - 2:
                done = slice(0, cols.stop) if c == len(chunks) - 2 else cols
                nc.sync.dma_start(out_words[:, done], y_codes[:, done].bitcast(I32))
        for q in range(PACK):
            queue = nc.scalar if q else nc.sync
            queue.dma_start(
                out_2[0, 4 * q : 4 * q + 4, :].bitcast(I32), y_sc[QUAD * q : QUAD * q + 4, :].bitcast(I32)
            )
